import numpy as np
import ml_dtypes


def mxq(x, axis, fmt="e4m3"):
    dtype, down = {"e4m3": (ml_dtypes.float8_e4m3fn, 7), "e5m2": (ml_dtypes.float8_e5m2, 14)}[fmt]
    v = np.moveaxis(np.asarray(x, np.float32).astype(ml_dtypes.bfloat16).astype(np.float64), axis, -1)
    blocks = v.reshape(v.shape[:-1] + (-1, 32))
    amax = np.abs(blocks).max(-1, keepdims=True)
    byte = np.maximum(np.where(amax > 0, np.frexp(amax)[1] - 1 + 127, 0) - down, 1)
    scale = np.exp2(byte - 127.0)
    codes = (blocks / scale).astype(np.float32).astype(dtype).astype(np.float64)
    return np.moveaxis((codes * scale).reshape(v.shape), -1, axis)


WIDE = False


def mx_kscale(k):
    if not WIDE:
        return np.ones(k)
    levels = np.array([10, -10, 5, -5, 0])
    if k % 512:
        return np.exp2(np.random.permutation(np.resize(levels, k // 32))).repeat(32)
    a = np.empty((k // 512, 16))
    for p in range(k // 512):
        a[p, :8] = np.random.permutation(np.resize(levels, 8))
        for g in range(8):
            far = levels[np.abs(levels - a[p, g]) >= 10]
            a[p, g + 8] = far[np.random.randint(len(far))]
    return np.exp2(a.ravel()).repeat(32)


def f64(x):
    return np.asarray(x).astype(np.float64)


def striped(idx):
    return np.tile(np.asarray(idx).reshape(-1, 16).T, (8, 1)).astype(np.uint16)


def unstriped(offs):
    return offs[:16].T.reshape(-1).astype(np.int64)


E2M1 = np.array([0.0, 0.5, 1.0, 1.5, 2.0, 3.0, 4.0, 6.0, -0.0, -0.5, -1.0, -1.5, -2.0, -3.0, -4.0, -6.0])


def pack_weight(w, fmt):
    k, n = w.shape
    w = f64(np.asarray(w, np.float32).astype(ml_dtypes.bfloat16)).reshape(k // 32, 32, n)
    amax = np.abs(w).max(1)
    if fmt == "e4m3":
        byte = np.frexp(amax)[1] - 1 + 127 - 7
    else:
        mant, ex = np.frexp(amax / 6.0)
        byte = np.where(mant > 0.5, ex, ex - 1) + 127
    byte = np.clip(np.where(amax > 0, byte, 1), 1, 254)
    scaled = (w * np.exp2(127.0 - byte)[:, None, :]).reshape(k, n).astype(np.float32)
    by_word = np.ascontiguousarray(scaled.reshape(k // 512, 128, 4, n).transpose(0, 1, 3, 2))
    if fmt == "e4m3":
        words = by_word.astype(ml_dtypes.float8_e4m3fn).view(np.uint8)
    else:
        c = by_word.astype(ml_dtypes.float4_e2m1fn).view(np.uint8) & 0xF
        words = (c[..., 0::2] | (c[..., 1::2] << 4)).reshape(k // 512, 128, 2 * n)
    return np.ascontiguousarray(words), np.ascontiguousarray(byte.astype(np.uint8).reshape(k // 512, 16, n))


def unpack_weight(words, scales, fmt):
    g, _, n = scales.shape
    words = np.ascontiguousarray(words).reshape(g, 128, n, -1)
    if fmt == "e4m3":
        vals = words.view(ml_dtypes.float8_e4m3fn).astype(np.float64)
    else:
        nib = np.empty((g, 128, n, 4), np.uint8)
        nib[..., 0::2] = words & 0xF
        nib[..., 1::2] = words >> 4
        vals = E2M1[nib]
    vals = vals * np.repeat(np.exp2(scales.astype(np.float64) - 127.0), 8, axis=1)[..., None]
    return vals.transpose(0, 1, 3, 2).reshape(g * 512, n)


D, E, T, I, Q = 512, 512, 2048, 512, 128


def setup_inputs():
    n = np.random.standard_normal
    idx = np.random.permutation(T)[:I]
    fd = mx_kscale(D)
    fe = mx_kscale(E)
    fi = mx_kscale(I)
    ti = np.ones(T)
    ti[idx] = fi
    keysp = pack_weight(n((D, T)) / fd[:, None], "e2m1")
    valsp = pack_weight(n((E, T)) / fe[:, None], "e2m1")
    return {
        "query": (n((D, Q)) * 0.6 / np.sqrt(D) * fd[:, None]).astype(np.float32),
        "keys_words": keysp[0],
        "keys_scales": keysp[1],
        "lprior": np.tile(np.random.uniform(-7.5, -5.0, T), (128, 1)).astype(np.float32),
        "strict": (np.random.uniform(0.2, 0.8, (Q, 1))).astype(np.float32),
        "gout": (n((E, Q)) * 1 / np.sqrt(E) * fe[:, None]).astype(np.float32),
        "vals_words": valsp[0],
        "vals_scales": valsp[1],
        "dquery": (n((D, Q)) * 1.0 / np.sqrt(D) * fd[:, None]).astype(np.float32),
        "fs": (np.random.uniform(128.0, 512.0, (1, I)) * fi).astype(np.float32),
        "keyrows": (n((D, T)) / ti).astype(np.float32),
        "res": (n((Q, D)) * 4.0).astype(np.float32),
        "offs": striped(idx),
    }


def reference(query, keys_words, keys_scales, lprior, strict, gout, vals_words, vals_scales, dquery, fs, keyrows, res, offs):
    idx = unstriped(offs)
    keysu = unpack_weight(keys_words, keys_scales, "e2m1")
    valsu = unpack_weight(vals_words, vals_scales, "e2m1")
    queryq = mxq(f64(query), 0, "e4m3")
    keysidxg = keysu[:, idx]
    a = queryq.T @ keysidxg
    dqueryq = mxq(f64(dquery), 0, "e4m3")
    ta = dqueryq.T @ keysidxg
    b = a - np.max(a, axis=1, keepdims=True)
    p = np.exp(b)
    z = np.sum(p, axis=1, keepdims=True)
    goutq = mxq(f64(gout), 0, "e4m3")
    valsidxg = valsu[:, idx]
    c0 = goutq.T @ valsidxg
    dz = f64(strict) / z - np.sum(p * c0, axis=1, keepdims=True) / np.square(z) - f64(strict) * (-1.0) * np.sum(p * (b - f64(lprior)[:1][:, idx]), axis=1, keepdims=True) / np.square(z)
    dp = 1.0 / z * c0 + f64(strict) * (-1.0) / z * (b - f64(lprior)[:1][:, idx]) + dz
    tb = ta
    tp = tb * p
    tz = np.sum(tp, axis=1, keepdims=True)
    tdz = tz * f64(strict) / np.square(z) * (-1.0) - (np.sum(tp * c0, axis=1, keepdims=True) - tz * z * 2.0 * np.sum(p * c0, axis=1, keepdims=True) / np.square(z)) / np.square(z) - (np.sum(tp * (b - f64(lprior)[:1][:, idx]) + tb * p, axis=1, keepdims=True) * f64(strict) * (-1.0) - tz * z * 2.0 * f64(strict) * (-1.0) * np.sum(p * (b - f64(lprior)[:1][:, idx]), axis=1, keepdims=True) / np.square(z)) / np.square(z)
    tdp = tz * 1.0 / np.square(z) * (-1.0) * c0 + tz * f64(strict) * (-1.0) / np.square(z) * (-1.0) * (b - f64(lprior)[:1][:, idx]) + tb * f64(strict) * (-1.0) / z + tdz
    tdb = tz * f64(strict) * (-1.0) / np.square(z) * (-1.0) * p + tp * f64(strict) * (-1.0) / z + tdp * p + tp * dp
    gs = tdb * f64(fs)
    gt1 = gs.T
    kt = f64(keyrows)[:, idx].T
    gt1q = mxq(gt1, 0, "e4m3")
    ktq = mxq(kt, 0, "e4m3")
    gq = gt1q.T @ ktq
    y = gq + f64(res)
    return y

@@ -1,0 +1,212 @@
+from contextlib import ExitStack
+
+import concourse.mybir as mybir
+from concourse.masks import make_identity
+
+D, E, T, I, Q = 512, 512, 2048, 512, 128
+FLOPS = 2 * Q * I * (2 * D + E + D)
+
+F32 = mybir.dt.float32
+BF16 = mybir.dt.bfloat16
+I32 = mybir.dt.int32
+U32 = mybir.dt.uint32
+U16 = mybir.dt.uint16
+U8 = mybir.dt.uint8
+FP8X4 = mybir.dt.float8_e4m3fn_x4
+FP4X4 = mybir.dt.float4_e2m1fn_x4
+ALU = mybir.AluOpType
+ACT = mybir.ActivationFunctionType
+
+P = 128
+PACK = 4
+PLANES = D // P
+
+
+def tile_attend_hvpriorpull_q_kernel(tc, query, keys_words, keys_scales, lprior, strict, gout, vals_words,
+                                      vals_scales, dquery, fs, keyrows, res, offs, out):
+    nc = tc.nc
+    with ExitStack() as ctx:
+        sb = ctx.enter_context(tc.tile_pool(name="sb", bufs=1))
+        ps = ctx.enter_context(tc.psum_pool(name="ps", bufs=1))
+        ps2 = ctx.enter_context(tc.psum_pool(name="ps2", bufs=4))
+
+        def tile(name, shape, dtype, tag=None):
+            return sb.tile(shape, dtype, name=name, tag=tag or name, align_bytes=64)
+
+        offsets = sb.tile([P, I // 16], U16, name="offsets")
+        kw = tile("kw", [P, T], U16)
+        vw = tile("vw", [P, T], U16)
+        ks = tile("ks", [P, T], U8)
+        vs = tile("vs", [P, T], U8)
+        q_raw = tile("q_raw", [P, PACK, Q], F32)
+        dq_raw = tile("dq_raw", [P, PACK, Q], F32)
+        go_raw = tile("go_raw", [P, PACK, Q], F32)
+        lp = tile("lp", [P, T], F32)
+        kr = [tile("kr%d" % j, [P, T], F32) for j in range(PLANES)]
+        res_sb = tile("res_sb", [P, D], F32)
+        s_col = tile("s_col", [P, 1], F32)
+        fs_col = tile("fs_col", [P, PACK], F32)
+        ident = tile("ident", [P, P], F32)
+
+        nc.gpsimd.memset(ks[:].bitcast(I32), 0)
+        nc.vector.memset(vs[:].bitcast(I32), 0)
+
+        def load_scales(eng, dst, src):
+            for quad in range(4):
+                eng.dma_start(out=dst[32 * quad:32 * quad + 4, :].bitcast(I32),
+                              in_=src[0, 4 * quad:4 * quad + 4, :].bitcast(I32))
+
+        nc.sync.dma_start(offsets[:], offs)
+        nc.sync.dma_start(out=kw[:].bitcast(I32), in_=keys_words[0].bitcast(I32))
+        load_scales(nc.sync, ks, keys_scales)
+        nc.sync.dma_start(out=q_raw[:], in_=query.rearrange("(p j) w -> p j w", j=PACK))
+        nc.sync.dma_start(out=dq_raw[:], in_=dquery.rearrange("(p j) w -> p j w", j=PACK))
+        nc.sync.dma_start(out=vw[:].bitcast(I32), in_=vals_words[0].bitcast(I32))
+        load_scales(nc.sync, vs, vals_scales)
+        nc.sync.dma_start(out=go_raw[:], in_=gout.rearrange("(p j) w -> p j w", j=PACK))
+        nc.sync.dma_start(out=lp[:], in_=lprior)
+        for j in range(PLANES):
+            nc.sync.dma_start(out=kr[j][:], in_=keyrows[P * j:P * (j + 1), :])
+        nc.sync.dma_start(out=res_sb[:], in_=res)
+        make_identity(nc, ident[:])
+        nc.gpsimd.dma_start(out=fs_col[:], in_=fs.rearrange("o (p t) -> (o p) t", t=PACK))
+        nc.gpsimd.dma_start(out=s_col[:], in_=strict)
+
+        warm = tile("warm", [P, 1], F32)
+        nc.vector.memset(warm[:], 0.0)
+        warm_out = tile("warm_out", [P, 1], F32)
+        nc.scalar.activation(out=warm_out[:], in_=warm[:], func=ACT.Exp)
+
+        kw_g = tile("kw_g", [P, I], U16)
+        ks_g = tile("ks_g", [P, I], U8)
+        vw_g = tile("vw_g", [P, I], U16)
+        vs_g = tile("vs_g", [P, I], U8)
+        nc.vector.tensor_copy(kw_g[:], kw[:].indirect(offsets[:]))
+        nc.vector.tensor_copy(ks_g[:], ks[:].indirect(offsets[:]))
+
+        qq = tile("qq", [P, 2, Q, PACK], BF16)
+        nc.scalar.copy(out=qq[:, 0], in_=q_raw[:].rearrange("p j w -> p w j"))
+        nc.scalar.copy(out=qq[:, 1], in_=dq_raw[:].rearrange("p j w -> p w j"))
+        qq_codes = tile("qq_codes", [P, 2 * Q], U32)
+        qq_scales = tile("qq_scales", [P, 2 * Q], U8)
+        nc.vector.quantize_mx(out=qq_codes[:].bitcast(FP8X4), scales=qq_scales[:],
+                              in_=qq[:].rearrange("p a w j -> p (a w j)"))
+
+        a_ps = ps.tile([P, I], F32, tag="bank_a", name="a_ps")
+        ta_ps = ps.tile([P, I], F32, tag="bank_ta", name="ta_ps")
+        c_ps = ps.tile([P, I], F32, tag="bank_c", name="c_ps")
+        for dst, half in ((a_ps, 0), (ta_ps, 1)):
+            nc.tensor.matmul_mx(out=dst[:], lhsT=qq_codes[:, half * Q:(half + 1) * Q].bitcast(FP8X4),
+                                lhsT_scale=qq_scales[:, half * Q:(half + 1) * Q],
+                                rhs=kw_g[:].bitcast(FP4X4), rhs_scale=ks_g[:], start=True, stop=True)
+
+        nc.vector.tensor_copy(vw_g[:], vw[:].indirect(offsets[:]))
+
+        neg_a = tile("neg_a", [P, I], F32)
+        neg_max = tile("neg_max", [P, 1], F32)
+        nc.vector.tensor_scalar(out=neg_a[:], in0=a_ps[:], scalar1=-1.0, scalar2=None, op0=ALU.mult, op1=ALU.min,
+                                accum_out=neg_max[:])
+        p_sb = tile("p_sb", [P, I], F32)
+        z = tile("z", [P, 1], F32)
+        nc.scalar.activation(out=p_sb[:], in_=a_ps[:], func=ACT.Exp, bias=neg_max[:], scale=1.0, accum_out=z[:])
+
+        nc.vector.tensor_copy(vs_g[:], vs[:].indirect(offsets[:]))
+        go = tile("go", [P, Q, PACK], BF16)
+        nc.scalar.copy(out=go[:], in_=go_raw[:].rearrange("p j w -> p w j"))
+        go_codes = tile("go_codes", [P, Q], U32)
+        go_scales = tile("go_scales", [P, Q], U8)
+        nc.vector.quantize_mx(out=go_codes[:].bitcast(FP8X4), scales=go_scales[:],
+                              in_=go[:].rearrange("p w j -> p (w j)"))
+        nc.tensor.matmul_mx(out=c_ps[:], lhsT=go_codes[:].bitcast(FP8X4), lhsT_scale=go_scales[:],
+                            rhs=vw_g[:].bitcast(FP4X4), rhs_scale=vs_g[:], start=True, stop=True)
+
+        r = tile("r", [P, 1], F32)
+        nc.vector.reciprocal(out=r[:], in_=z[:])
+        pi = tile("pi", [P, I], F32)
+        nc.scalar.activation(out=pi[:], in_=p_sb[:], func=ACT.Copy, scale=r[:])
+
+        nu = tile("nu", [P, I], F32)
+        nc.vector.tensor_tensor(nu[:], lp[:].indirect(offsets[:]), neg_a[:], ALU.add)
+
+        g = tile("g", [P, I], F32)
+        nc.vector.scalar_tensor_tensor(out=g[:], in0=nu[:], scalar=s_col[:], in1=c_ps[:], op0=ALU.mult, op1=ALU.add)
+        pi_ta = tile("pi_ta", [P, I], F32)
+        m = tile("m", [P, 1], F32)
+        nc.vector.scalar_tensor_tensor(out=pi_ta[:], in0=ta_ps[:], scalar=1.0, in1=pi[:], op0=ALU.mult,
+                                       op1=ALU.mult, accum_out=m[:])
+        pi_g = tile("pi_g", [P, I], F32)
+        g_bar = tile("g_bar", [P, 1], F32)
+        nc.vector.scalar_tensor_tensor(out=pi_g[:], in0=g[:], scalar=1.0, in1=pi[:], op0=ALU.mult,
+                                       op1=ALU.mult, accum_out=g_bar[:])
+        w = tile("w", [P, I], F32)
+        cov = tile("cov", [P, 1], F32)
+        nc.vector.scalar_tensor_tensor(out=w[:], in0=ta_ps[:], scalar=m[:], in1=pi_g[:], op0=ALU.subtract,
+                                       op1=ALU.mult, accum_out=cov[:])
+        neg_s = tile("neg_s", [P, 1], F32)
+        nc.gpsimd.tensor_scalar(out=neg_s[:], in0=s_col[:], scalar1=-1.0, scalar2=0.0, op0=ALU.mult, op1=ALU.add)
+        neg_k = tile("neg_k", [P, 1], F32)
+        nc.scalar.activation(out=neg_k[:], in_=g_bar[:], func=ACT.Identity, bias=neg_s[:], scale=-1.0)
+        km = tile("km", [P, 1], F32)
+        nc.gpsimd.tensor_scalar(out=km[:], in0=g_bar[:], scalar1=s_col[:], scalar2=m[:], op0=ALU.add, op1=ALU.mult)
+        term_ta = tile("term_ta", [P, PACK, P], F32)
+        nc.scalar.activation(out=term_ta[:].rearrange("p t s -> p s t"),
+                             in_=pi_ta[:].rearrange("p (s t) -> p s t", t=PACK), func=ACT.Copy, scale=neg_k[:])
+        coef = tile("coef", [P, 1], F32)
+        nc.scalar.activation(out=coef[:], in_=cov[:], func=ACT.Identity, bias=km[:], scale=-1.0)
+        term_pi = tile("term_pi", [P, PACK, P], F32)
+        nc.scalar.activation(out=term_pi[:].rearrange("p t s -> p s t"),
+                             in_=pi[:].rearrange("p (s t) -> p s t", t=PACK), func=ACT.Copy, scale=coef[:])
+
+        def slots_to_partitions(src_bf16, grouped, name):
+            bank = ps2.tile([P, 2, P], F32, tag="bank_turn", name=name + "_ps")
+            words = src_bf16[:].bitcast(F32)
+            for u in range(2):
+                nc.tensor.transpose(bank[:, u, :], words[:, u::2], ident[:])
+            nc.scalar.copy(out=grouped.bitcast(F32), in_=bank[:].rearrange("p u r -> p r u"))
+
+        def quantise(grouped, name, tag):
+            width = grouped.shape[1] * P
+            codes = tile(name + "_codes", [P, width], U32, tag=tag)
+            scales = tile(name + "_scales", [P, width], U8)
+            nc.vector.quantize_mx(out=codes[:].bitcast(FP8X4), scales=scales[:],
+                                  in_=grouped[:].rearrange("p a r t -> p (a r t)"))
+            return codes, scales
+
+        def key_plane(j, grouped):
+            kt = tile("kt%d" % j, [P, I], BF16)
+            nc.vector.tensor_copy(kt[:], kr[j][:].indirect(offsets[:]))
+            slots_to_partitions(kt, grouped, "kt%d" % j)
+
+        first = tile("first", [P, 4, P, PACK], BF16)
+        last = tile("last", [P, 1, P, PACK], BF16)
+        tdb_ps = [ps.tile([P, P], F32, tag=tag, name="tdb_ps%d" % t)
+                  for t, tag in enumerate(("bank_a", "bank_c", "bank_x", "bank_ta"))]
+        for t in range(PACK):
+            nc.tensor.matmul(tdb_ps[t][:], term_ta[:, t, :], ident[:], is_transpose=True, start=True, stop=False)
+        for t in range(PACK):
+            nc.tensor.matmul(tdb_ps[t][:], w[:, t::PACK], ident[:], is_transpose=True, start=False, stop=False)
+        for t in range(PACK):
+            nc.tensor.matmul(tdb_ps[t][:], term_pi[:, t, :], ident[:], is_transpose=True, start=False, stop=True)
+            nc.scalar.activation(out=first[:, 0, :, t], in_=tdb_ps[t][:], func=ACT.Copy, scale=fs_col[:, t:t + 1])
+        for j in range(PLANES - 1):
+            key_plane(j, first[:, 1 + j])
+        key_plane(PLANES - 1, last[:, 0])
+        first_codes, first_scales = quantise(first, "first", "kr3")
+        last_codes, last_scales = quantise(last, "last", None)
+
+        def product(acc, codes, scales):
+            nc.tensor.matmul_mx(out=acc, lhsT=first_codes[:, 0:P].bitcast(FP8X4), lhsT_scale=first_scales[:, 0:P],
+                                rhs=codes.bitcast(FP8X4), rhs_scale=scales, start=True, stop=True)
+
+        def finish(acc, cols, name):
+            y = tile(name, [P, cols.stop - cols.start], F32)
+            nc.vector.tensor_tensor(out=y[:], in0=acc[:], in1=res_sb[:, cols], op=ALU.add)
+            nc.sync.dma_start(out=out[:, cols], in_=y[:])
+
+        acc_head = ps.tile([P, 3 * P], F32, tag="bank_a", name="acc_head")
+        product(acc_head[:, 0:P], first_codes[:, P:2 * P], first_scales[:, P:2 * P])
+        product(acc_head[:, P:3 * P], first_codes[:, 2 * P:4 * P], first_scales[:, 2 * P:4 * P])
+        finish(acc_head, slice(0, 3 * P), "y_head")
+        acc_tail = ps.tile([P, P], F32, tag="bank_c", name="acc_tail")
+        product(acc_tail[:], last_codes[:], last_scales[:])
+        finish(acc_tail, slice(3 * P, D), "y_tail")

@@ -41,7 +41,6 @@ def tile_attend_hvpriorpull_q_kernel(tc, query, keys_words, keys_scales, lprior,
         q_raw = tile("q_raw", [P, PACK, Q], F32)
         dq_raw = tile("dq_raw", [P, PACK, Q], F32)
         go_raw = tile("go_raw", [P, PACK, Q], F32)
-        lp = tile("lp", [P, T], F32)
         kr = [tile("kr%d" % j, [P, T], F32) for j in range(PLANES)]
         res_sb = tile("res_sb", [P, D], F32)
         s_col = tile("s_col", [P, 1], F32)
@@ -52,25 +51,26 @@ def tile_attend_hvpriorpull_q_kernel(tc, query, keys_words, keys_scales, lprior,
         nc.vector.memset(vs[:].bitcast(I32), 0)
 
         def load_scales(eng, dst, src):
-            for quad in range(4):
-                eng.dma_start(out=dst[32 * quad:32 * quad + 4, :].bitcast(I32),
-                              in_=src[0, 4 * quad:4 * quad + 4, :].bitcast(I32))
+            for row in range(4):
+                eng.dma_start(out=dst[row:P:32, :].bitcast(I32), in_=src[0, row::4, :].bitcast(I32))
 
         nc.sync.dma_start(offsets[:], offs)
-        nc.sync.dma_start(out=kw[:].bitcast(I32), in_=keys_words[0].bitcast(I32))
         load_scales(nc.sync, ks, keys_scales)
+        lp_cols = tile("lp_cols", [P, T // P], F32)
+        nc.sync.dma_start(out=lp_cols[:], in_=lprior[0:1, :].rearrange("o (p c) -> (o p) c", p=P))
+        nc.sync.dma_start(out=kw[:].bitcast(I32), in_=keys_words[0].bitcast(I32))
         nc.sync.dma_start(out=q_raw[:], in_=query.rearrange("(p j) w -> p j w", j=PACK))
         nc.sync.dma_start(out=dq_raw[:], in_=dquery.rearrange("(p j) w -> p j w", j=PACK))
-        nc.sync.dma_start(out=vw[:].bitcast(I32), in_=vals_words[0].bitcast(I32))
         load_scales(nc.sync, vs, vals_scales)
+        nc.sync.dma_start(out=vw[:].bitcast(I32), in_=vals_words[0].bitcast(I32))
         nc.sync.dma_start(out=go_raw[:], in_=gout.rearrange("(p j) w -> p j w", j=PACK))
-        nc.sync.dma_start(out=lp[:], in_=lprior)
-        for j in range(PLANES):
+        nc.sync.dma_start(out=kr[0][:], in_=keyrows[0:P, :])
+        nc.sync.dma_start(out=s_col[:], in_=strict)
+        nc.sync.dma_start(out=fs_col[:], in_=fs.rearrange("o (p t) -> (o p) t", t=PACK))
+        for j in range(1, PLANES):
             nc.sync.dma_start(out=kr[j][:], in_=keyrows[P * j:P * (j + 1), :])
         nc.sync.dma_start(out=res_sb[:], in_=res)
         make_identity(nc, ident[:])
-        nc.gpsimd.dma_start(out=fs_col[:], in_=fs.rearrange("o (p t) -> (o p) t", t=PACK))
-        nc.gpsimd.dma_start(out=s_col[:], in_=strict)
 
         warm = tile("warm", [P, 1], F32)
         nc.vector.memset(warm[:], 0.0)
@@ -80,9 +80,8 @@ def tile_attend_hvpriorpull_q_kernel(tc, query, keys_words, keys_scales, lprior,
         kw_g = tile("kw_g", [P, I], U16)
         ks_g = tile("ks_g", [P, I], U8)
         vw_g = tile("vw_g", [P, I], U16)
-        vs_g = tile("vs_g", [P, I], U8)
-        nc.vector.tensor_copy(kw_g[:], kw[:].indirect(offsets[:]))
         nc.vector.tensor_copy(ks_g[:], ks[:].indirect(offsets[:]))
+        nc.vector.tensor_copy(kw_g[:], kw[:].indirect(offsets[:]))
 
         qq = tile("qq", [P, 2, Q, PACK], BF16)
         nc.scalar.copy(out=qq[:, 0], in_=q_raw[:].rearrange("p j w -> p w j"))
@@ -92,6 +91,16 @@ def tile_attend_hvpriorpull_q_kernel(tc, query, keys_words, keys_scales, lprior,
         nc.vector.quantize_mx(out=qq_codes[:].bitcast(FP8X4), scales=qq_scales[:],
                               in_=qq[:].rearrange("p a w j -> p (a w j)"))
 
+        lp = tile("lp", [P, T], F32, tag="dq_raw")
+        lp_view = lp[:].rearrange("p (n c) -> p n c", n=P)
+        for b in range(T // P // PACK):
+            lp_ps = ps2.tile([P, PACK, P], F32, tag="bank_turn", name="lp_ps%d" % b)
+            for c in range(PACK):
+                col = PACK * b + c
+                nc.tensor.transpose(lp_ps[:, c, :], lp_cols[:, col:col + 1].to_broadcast([P, P]), ident[:])
+            nc.scalar.activation(out=lp_view[:, :, PACK * b:PACK * (b + 1)], in_=lp_ps[:].rearrange("p c n -> p n c"),
+                                 func=ACT.Copy)
+
         a_ps = ps.tile([P, I], F32, tag="bank_a", name="a_ps")
         ta_ps = ps.tile([P, I], F32, tag="bank_ta", name="ta_ps")
         c_ps = ps.tile([P, I], F32, tag="bank_c", name="c_ps")
@@ -100,8 +109,12 @@ def tile_attend_hvpriorpull_q_kernel(tc, query, keys_words, keys_scales, lprior,
                                 lhsT_scale=qq_scales[:, half * Q:(half + 1) * Q],
                                 rhs=kw_g[:].bitcast(FP4X4), rhs_scale=ks_g[:], start=True, stop=True)
 
+        vs_g = tile("vs_g", [P, I], U8, tag="qq")
+        nc.vector.tensor_copy(vs_g[:], vs[:].indirect(offsets[:]))
         nc.vector.tensor_copy(vw_g[:], vw[:].indirect(offsets[:]))
 
+        go = tile("go", [P, Q, PACK], BF16)
+        nc.scalar.copy(out=go[:], in_=go_raw[:].rearrange("p j w -> p w j"))
         neg_a = tile("neg_a", [P, I], F32)
         neg_max = tile("neg_max", [P, 1], F32)
         nc.vector.tensor_scalar(out=neg_a[:], in0=a_ps[:], scalar1=-1.0, scalar2=None, op0=ALU.mult, op1=ALU.min,
@@ -110,52 +123,12 @@ def tile_attend_hvpriorpull_q_kernel(tc, query, keys_words, keys_scales, lprior,
         z = tile("z", [P, 1], F32)
         nc.scalar.activation(out=p_sb[:], in_=a_ps[:], func=ACT.Exp, bias=neg_max[:], scale=1.0, accum_out=z[:])
 
-        nc.vector.tensor_copy(vs_g[:], vs[:].indirect(offsets[:]))
-        go = tile("go", [P, Q, PACK], BF16)
-        nc.scalar.copy(out=go[:], in_=go_raw[:].rearrange("p j w -> p w j"))
         go_codes = tile("go_codes", [P, Q], U32)
         go_scales = tile("go_scales", [P, Q], U8)
         nc.vector.quantize_mx(out=go_codes[:].bitcast(FP8X4), scales=go_scales[:],
                               in_=go[:].rearrange("p w j -> p (w j)"))
         nc.tensor.matmul_mx(out=c_ps[:], lhsT=go_codes[:].bitcast(FP8X4), lhsT_scale=go_scales[:],
                             rhs=vw_g[:].bitcast(FP4X4), rhs_scale=vs_g[:], start=True, stop=True)
-
-        r = tile("r", [P, 1], F32)
-        nc.vector.reciprocal(out=r[:], in_=z[:])
-        pi = tile("pi", [P, I], F32)
-        nc.scalar.activation(out=pi[:], in_=p_sb[:], func=ACT.Copy, scale=r[:])
-
-        nu = tile("nu", [P, I], F32)
-        nc.vector.tensor_tensor(nu[:], lp[:].indirect(offsets[:]), neg_a[:], ALU.add)
-
-        g = tile("g", [P, I], F32)
-        nc.vector.scalar_tensor_tensor(out=g[:], in0=nu[:], scalar=s_col[:], in1=c_ps[:], op0=ALU.mult, op1=ALU.add)
-        pi_ta = tile("pi_ta", [P, I], F32)
-        m = tile("m", [P, 1], F32)
-        nc.vector.scalar_tensor_tensor(out=pi_ta[:], in0=ta_ps[:], scalar=1.0, in1=pi[:], op0=ALU.mult,
-                                       op1=ALU.mult, accum_out=m[:])
-        pi_g = tile("pi_g", [P, I], F32)
-        g_bar = tile("g_bar", [P, 1], F32)
-        nc.vector.scalar_tensor_tensor(out=pi_g[:], in0=g[:], scalar=1.0, in1=pi[:], op0=ALU.mult,
-                                       op1=ALU.mult, accum_out=g_bar[:])
-        w = tile("w", [P, I], F32)
-        cov = tile("cov", [P, 1], F32)
-        nc.vector.scalar_tensor_tensor(out=w[:], in0=ta_ps[:], scalar=m[:], in1=pi_g[:], op0=ALU.subtract,
-                                       op1=ALU.mult, accum_out=cov[:])
-        neg_s = tile("neg_s", [P, 1], F32)
-        nc.gpsimd.tensor_scalar(out=neg_s[:], in0=s_col[:], scalar1=-1.0, scalar2=0.0, op0=ALU.mult, op1=ALU.add)
-        neg_k = tile("neg_k", [P, 1], F32)
-        nc.scalar.activation(out=neg_k[:], in_=g_bar[:], func=ACT.Identity, bias=neg_s[:], scale=-1.0)
-        km = tile("km", [P, 1], F32)
-        nc.gpsimd.tensor_scalar(out=km[:], in0=g_bar[:], scalar1=s_col[:], scalar2=m[:], op0=ALU.add, op1=ALU.mult)
-        term_ta = tile("term_ta", [P, PACK, P], F32)
-        nc.scalar.activation(out=term_ta[:].rearrange("p t s -> p s t"),
-                             in_=pi_ta[:].rearrange("p (s t) -> p s t", t=PACK), func=ACT.Copy, scale=neg_k[:])
-        coef = tile("coef", [P, 1], F32)
-        nc.scalar.activation(out=coef[:], in_=cov[:], func=ACT.Identity, bias=km[:], scale=-1.0)
-        term_pi = tile("term_pi", [P, PACK, P], F32)
-        nc.scalar.activation(out=term_pi[:].rearrange("p t s -> p s t"),
-                             in_=pi[:].rearrange("p (s t) -> p s t", t=PACK), func=ACT.Copy, scale=coef[:])
 
         def slots_to_partitions(src_bf16, grouped, name):
             bank = ps2.tile([P, 2, P], F32, tag="bank_turn", name=name + "_ps")
@@ -172,24 +145,64 @@ def tile_attend_hvpriorpull_q_kernel(tc, query, keys_words, keys_scales, lprior,
                                   in_=grouped[:].rearrange("p a r t -> p (a r t)"))
             return codes, scales
 
-        def key_plane(j, grouped):
-            kt = tile("kt%d" % j, [P, I], BF16)
+        def key_plane(j, grouped, tag=None):
+            kt = tile("kt%d" % j, [P, I], BF16, tag=tag)
             nc.vector.tensor_copy(kt[:], kr[j][:].indirect(offsets[:]))
             slots_to_partitions(kt, grouped, "kt%d" % j)
 
-        first = tile("first", [P, 4, P, PACK], BF16)
+        r = tile("r", [P, 1], F32)
+        nc.vector.reciprocal(out=r[:], in_=z[:])
+        nu = tile("nu", [P, I], F32)
+        nc.vector.tensor_tensor(nu[:], lp[:].indirect(offsets[:]), neg_a[:], ALU.add)
+        pi_ta = tile("pi_ta", [P, I], F32)
+        m = tile("m", [P, 1], F32)
+        nc.vector.scalar_tensor_tensor(out=pi_ta[:], in0=ta_ps[:], scalar=r[:], in1=p_sb[:], op0=ALU.mult,
+                                       op1=ALU.mult, accum_out=m[:])
+        g = tile("g", [P, I], F32)
+        nc.vector.scalar_tensor_tensor(out=g[:], in0=nu[:], scalar=s_col[:], in1=c_ps[:], op0=ALU.mult, op1=ALU.add)
+        pi_g = tile("pi_g", [P, I], F32)
+        g_bar = tile("g_bar", [P, 1], F32)
+        nc.vector.scalar_tensor_tensor(out=pi_g[:], in0=g[:], scalar=r[:], in1=p_sb[:], op0=ALU.mult,
+                                       op1=ALU.mult, accum_out=g_bar[:])
         last = tile("last", [P, 1, P, PACK], BF16)
+        kr0_bf16 = tile("kr0_bf16", [P, T], BF16)
+        nc.scalar.activation(out=kr0_bf16[:], in_=kr[0][:], func=ACT.Copy)
+        kt0 = tile("kt0", [P, I], BF16)
+        nc.scalar.activation(out=kt0[:], in_=kr0_bf16[:].indirect(offsets[:]), func=ACT.Copy)
+        neg_r = tile("neg_r", [P, 1], F32)
+        nc.gpsimd.tensor_scalar(out=neg_r[:], in0=r[:], scalar1=-1.0, scalar2=0.0, op0=ALU.mult, op1=ALU.add)
+        mr = tile("mr", [P, 1], F32)
+        nc.gpsimd.tensor_scalar(out=mr[:], in0=m[:], scalar1=r[:], scalar2=0.0, op0=ALU.mult, op1=ALU.add)
+        neg_k = tile("neg_k", [P, 1], F32)
+        nc.vector.tensor_scalar(out=neg_k[:], in0=g_bar[:], scalar1=s_col[:], scalar2=-1.0, op0=ALU.add, op1=ALU.mult)
+        kmr = tile("kmr", [P, 1], F32)
+        nc.vector.tensor_scalar(out=kmr[:], in0=g_bar[:], scalar1=s_col[:], scalar2=mr[:], op0=ALU.add, op1=ALU.mult)
+        w = tile("w", [P, I], F32)
+        cov = tile("cov", [P, 1], F32)
+        nc.vector.scalar_tensor_tensor(out=w[:], in0=ta_ps[:], scalar=m[:], in1=pi_g[:], op0=ALU.subtract,
+                                       op1=ALU.mult, accum_out=cov[:])
+        term_ta = tile("term_ta", [P, PACK, P], F32)
+        nc.scalar.activation(out=term_ta[:].rearrange("p t s -> p s t"),
+                             in_=pi_ta[:].rearrange("p (s t) -> p s t", t=PACK), func=ACT.Copy, scale=neg_k[:])
+        coef = tile("coef", [P, 1], F32)
+        nc.scalar.activation(out=coef[:], in_=cov[:], func=ACT.Identity, bias=kmr[:], scale=neg_r[:])
+        term_pi = tile("term_pi", [P, PACK, P], F32)
+        nc.scalar.activation(out=term_pi[:].rearrange("p t s -> p s t"),
+                             in_=p_sb[:].rearrange("p (s t) -> p s t", t=PACK), func=ACT.Copy, scale=coef[:])
+
+        first = tile("first", [P, 4, P, PACK], BF16, tag="p_sb")
+        slots_to_partitions(kt0, first[:, 1], "kt0")
         tdb_ps = [ps.tile([P, P], F32, tag=tag, name="tdb_ps%d" % t)
                   for t, tag in enumerate(("bank_a", "bank_c", "bank_x", "bank_ta"))]
         for t in range(PACK):
-            nc.tensor.matmul(tdb_ps[t][:], term_ta[:, t, :], ident[:], is_transpose=True, start=True, stop=False)
+            nc.tensor.matmul(tdb_ps[t][:], w[:, t::PACK], ident[:], is_transpose=True, start=True, stop=False)
         for t in range(PACK):
-            nc.tensor.matmul(tdb_ps[t][:], w[:, t::PACK], ident[:], is_transpose=True, start=False, stop=False)
+            nc.tensor.matmul(tdb_ps[t][:], term_ta[:, t, :], ident[:], is_transpose=True, start=False, stop=False)
         for t in range(PACK):
             nc.tensor.matmul(tdb_ps[t][:], term_pi[:, t, :], ident[:], is_transpose=True, start=False, stop=True)
             nc.scalar.activation(out=first[:, 0, :, t], in_=tdb_ps[t][:], func=ACT.Copy, scale=fs_col[:, t:t + 1])
-        for j in range(PLANES - 1):
-            key_plane(j, first[:, 1 + j])
+        key_plane(1, first[:, 2], "pi_g")
+        key_plane(2, first[:, 3])
         key_plane(PLANES - 1, last[:, 0])
         first_codes, first_scales = quantise(first, "first", "kr3")
         last_codes, last_scales = quantise(last, "last", None)
@@ -198,15 +211,15 @@ def tile_attend_hvpriorpull_q_kernel(tc, query, keys_words, keys_scales, lprior,
             nc.tensor.matmul_mx(out=acc, lhsT=first_codes[:, 0:P].bitcast(FP8X4), lhsT_scale=first_scales[:, 0:P],
                                 rhs=codes.bitcast(FP8X4), rhs_scale=scales, start=True, stop=True)
 
-        def finish(acc, cols, name):
-            y = tile(name, [P, cols.stop - cols.start], F32)
+        def finish(acc, cols, name, tag=None):
+            y = tile(name, [P, cols.stop - cols.start], F32, tag=tag)
             nc.vector.tensor_tensor(out=y[:], in0=acc[:], in1=res_sb[:, cols], op=ALU.add)
             nc.sync.dma_start(out=out[:, cols], in_=y[:])
 
         acc_head = ps.tile([P, 3 * P], F32, tag="bank_a", name="acc_head")
         product(acc_head[:, 0:P], first_codes[:, P:2 * P], first_scales[:, P:2 * P])
         product(acc_head[:, P:3 * P], first_codes[:, 2 * P:4 * P], first_scales[:, 2 * P:4 * P])
-        finish(acc_head, slice(0, 3 * P), "y_head")
+        finish(acc_head, slice(0, 3 * P), "y_head", "last")
         acc_tail = ps.tile([P, P], F32, tag="bank_c", name="acc_tail")
         product(acc_tail[:], last_codes[:], last_scales[:])
         finish(acc_tail, slice(3 * P, D), "y_tail")

@@ -119,9 +119,12 @@ def tile_attend_hvpriorpull_q_kernel(tc, query, keys_words, keys_scales, lprior,
         neg_max = tile("neg_max", [P, 1], F32)
         nc.vector.tensor_scalar(out=neg_a[:], in0=a_ps[:], scalar1=-1.0, scalar2=None, op0=ALU.mult, op1=ALU.min,
                                 accum_out=neg_max[:])
+        p_dealt = tile("p_dealt", [P, PACK, P], F32)
         p_sb = tile("p_sb", [P, I], F32)
         z = tile("z", [P, 1], F32)
-        nc.scalar.activation(out=p_sb[:], in_=a_ps[:], func=ACT.Exp, bias=neg_max[:], scale=1.0, accum_out=z[:])
+        nc.scalar.activation(out=p_dealt[:], in_=a_ps[:].rearrange("p (s t) -> p t s", t=PACK), func=ACT.Exp,
+                             bias=neg_max[:], scale=1.0, accum_out=z[:])
+        nc.scalar.activation(out=p_sb[:], in_=a_ps[:], func=ACT.Exp, bias=neg_max[:], scale=1.0)
 
         go_codes = tile("go_codes", [P, Q], U32)
         go_scales = tile("go_scales", [P, Q], U8)
@@ -154,10 +157,10 @@ def tile_attend_hvpriorpull_q_kernel(tc, query, keys_words, keys_scales, lprior,
         nc.vector.reciprocal(out=r[:], in_=z[:])
         nu = tile("nu", [P, I], F32)
         nc.vector.tensor_tensor(nu[:], lp[:].indirect(offsets[:]), neg_a[:], ALU.add)
-        pi_ta = tile("pi_ta", [P, I], F32)
+        pi_ta = tile("pi_ta", [P, PACK, P], F32)
         m = tile("m", [P, 1], F32)
-        nc.vector.scalar_tensor_tensor(out=pi_ta[:], in0=ta_ps[:], scalar=r[:], in1=p_sb[:], op0=ALU.mult,
-                                       op1=ALU.mult, accum_out=m[:])
+        nc.vector.scalar_tensor_tensor(out=pi_ta[:], in0=ta_ps[:].rearrange("p (s t) -> p t s", t=PACK), scalar=r[:],
+                                       in1=p_dealt[:], op0=ALU.mult, op1=ALU.mult, accum_out=m[:])
         g = tile("g", [P, I], F32)
         nc.vector.scalar_tensor_tensor(out=g[:], in0=nu[:], scalar=s_col[:], in1=c_ps[:], op0=ALU.mult, op1=ALU.add)
         pi_g = tile("pi_g", [P, I], F32)
@@ -182,16 +185,15 @@ def tile_attend_hvpriorpull_q_kernel(tc, query, keys_words, keys_scales, lprior,
         nc.vector.scalar_tensor_tensor(out=w[:], in0=ta_ps[:], scalar=m[:], in1=pi_g[:], op0=ALU.subtract,
                                        op1=ALU.mult, accum_out=cov[:])
         term_ta = tile("term_ta", [P, PACK, P], F32)
-        nc.scalar.activation(out=term_ta[:].rearrange("p t s -> p s t"),
-                             in_=pi_ta[:].rearrange("p (s t) -> p s t", t=PACK), func=ACT.Copy, scale=neg_k[:])
+        nc.scalar.activation(out=term_ta[:], in_=pi_ta[:], func=ACT.Copy, scale=neg_k[:])
         coef = tile("coef", [P, 1], F32)
         nc.scalar.activation(out=coef[:], in_=cov[:], func=ACT.Identity, bias=kmr[:], scale=neg_r[:])
         term_pi = tile("term_pi", [P, PACK, P], F32)
-        nc.scalar.activation(out=term_pi[:].rearrange("p t s -> p s t"),
-                             in_=p_sb[:].rearrange("p (s t) -> p s t", t=PACK), func=ACT.Copy, scale=coef[:])
+        nc.scalar.activation(out=term_pi[:], in_=p_dealt[:], func=ACT.Copy, scale=coef[:])
 
-        first = tile("first", [P, 4, P, PACK], BF16, tag="p_sb")
+        first = tile("first", [P, 4, P, PACK], BF16, tag="p_dealt")
         slots_to_partitions(kt0, first[:, 1], "kt0")
+        gt1 = tile("gt1", [P, PACK, Q], BF16)
         tdb_ps = [ps.tile([P, P], F32, tag=tag, name="tdb_ps%d" % t)
                   for t, tag in enumerate(("bank_a", "bank_c", "bank_x", "bank_ta"))]
         for t in range(PACK):
@@ -200,7 +202,8 @@ def tile_attend_hvpriorpull_q_kernel(tc, query, keys_words, keys_scales, lprior,
             nc.tensor.matmul(tdb_ps[t][:], term_ta[:, t, :], ident[:], is_transpose=True, start=False, stop=False)
         for t in range(PACK):
             nc.tensor.matmul(tdb_ps[t][:], term_pi[:, t, :], ident[:], is_transpose=True, start=False, stop=True)
-            nc.scalar.activation(out=first[:, 0, :, t], in_=tdb_ps[t][:], func=ACT.Copy, scale=fs_col[:, t:t + 1])
+            nc.scalar.activation(out=gt1[:, t, :], in_=tdb_ps[t][:], func=ACT.Copy, scale=fs_col[:, t:t + 1])
+        nc.scalar.copy(out=first[:, 0], in_=gt1[:].rearrange("p t q -> p q t"))
         key_plane(1, first[:, 2], "pi_g")
         key_plane(2, first[:, 3])
         key_plane(PLANES - 1, last[:, 0])

from contextlib import ExitStack

import concourse.mybir as mybir
from concourse.masks import make_identity

D, E, T, I, Q = 512, 512, 2048, 512, 128
FLOPS = 2 * Q * I * (2 * D + E + D)

F32 = mybir.dt.float32
BF16 = mybir.dt.bfloat16
I32 = mybir.dt.int32
U32 = mybir.dt.uint32
U16 = mybir.dt.uint16
U8 = mybir.dt.uint8
FP8X4 = mybir.dt.float8_e4m3fn_x4
FP4X4 = mybir.dt.float4_e2m1fn_x4
ALU = mybir.AluOpType
ACT = mybir.ActivationFunctionType

P = 128
PACK = 4
PLANES = D // P


def tile_attend_hvpriorpull_q_kernel(tc, query, keys_words, keys_scales, lprior, strict, gout, vals_words,
                                      vals_scales, dquery, fs, keyrows, res, offs, out):
    nc = tc.nc
    with ExitStack() as ctx:
        sb = ctx.enter_context(tc.tile_pool(name="sb", bufs=1))
        ps = ctx.enter_context(tc.psum_pool(name="ps", bufs=1))
        ps2 = ctx.enter_context(tc.psum_pool(name="ps2", bufs=4))

        def tile(name, shape, dtype, tag=None):
            return sb.tile(shape, dtype, name=name, tag=tag or name, align_bytes=64)

        offsets = sb.tile([P, I // 16], U16, name="offsets")
        kw = tile("kw", [P, T], U16)
        vw = tile("vw", [P, T], U16)
        ks = tile("ks", [P, T], U8)
        vs = tile("vs", [P, T], U8)
        q_raw = tile("q_raw", [P, PACK, Q], F32)
        dq_raw = tile("dq_raw", [P, PACK, Q], F32)
        go_raw = tile("go_raw", [P, PACK, Q], F32)
        kr = [tile("kr%d" % j, [P, T], F32) for j in range(PLANES)]
        res_sb = tile("res_sb", [P, D], F32)
        s_col = tile("s_col", [P, 1], F32)
        fs_col = tile("fs_col", [P, PACK], F32)
        ident = tile("ident", [P, P], F32)

        nc.gpsimd.memset(ks[:].bitcast(I32), 0)
        nc.vector.memset(vs[:].bitcast(I32), 0)

        def load_scales(eng, dst, src):
            for row in range(4):
                eng.dma_start(out=dst[row:P:32, :].bitcast(I32), in_=src[0, row::4, :].bitcast(I32))

        nc.sync.dma_start(offsets[:], offs)
        load_scales(nc.sync, ks, keys_scales)
        lp_cols = tile("lp_cols", [P, T // P], F32)
        nc.sync.dma_start(out=lp_cols[:], in_=lprior[0:1, :].rearrange("o (p c) -> (o p) c", p=P))
        nc.sync.dma_start(out=kw[:].bitcast(I32), in_=keys_words[0].bitcast(I32))
        nc.sync.dma_start(out=q_raw[:], in_=query.rearrange("(p j) w -> p j w", j=PACK))
        nc.sync.dma_start(out=dq_raw[:], in_=dquery.rearrange("(p j) w -> p j w", j=PACK))
        load_scales(nc.sync, vs, vals_scales)
        nc.sync.dma_start(out=vw[:].bitcast(I32), in_=vals_words[0].bitcast(I32))
        nc.sync.dma_start(out=go_raw[:], in_=gout.rearrange("(p j) w -> p j w", j=PACK))
        nc.sync.dma_start(out=kr[0][:], in_=keyrows[0:P, :])
        nc.sync.dma_start(out=s_col[:], in_=strict)
        nc.sync.dma_start(out=fs_col[:], in_=fs.rearrange("o (p t) -> (o p) t", t=PACK))
        for j in range(1, PLANES):
            nc.sync.dma_start(out=kr[j][:], in_=keyrows[P * j:P * (j + 1), :])
        nc.sync.dma_start(out=res_sb[:], in_=res)
        make_identity(nc, ident[:])

        warm = tile("warm", [P, 1], F32)
        nc.vector.memset(warm[:], 0.0)
        warm_out = tile("warm_out", [P, 1], F32)
        nc.scalar.activation(out=warm_out[:], in_=warm[:], func=ACT.Exp)

        kw_g = tile("kw_g", [P, I], U16)
        ks_g = tile("ks_g", [P, I], U8)
        vw_g = tile("vw_g", [P, I], U16)
        nc.vector.tensor_copy(ks_g[:], ks[:].indirect(offsets[:]))
        nc.vector.tensor_copy(kw_g[:], kw[:].indirect(offsets[:]))

        qq = tile("qq", [P, 2, Q, PACK], BF16)
        nc.scalar.copy(out=qq[:, 0], in_=q_raw[:].rearrange("p j w -> p w j"))
        nc.scalar.copy(out=qq[:, 1], in_=dq_raw[:].rearrange("p j w -> p w j"))
        qq_codes = tile("qq_codes", [P, 2 * Q], U32)
        qq_scales = tile("qq_scales", [P, 2 * Q], U8)
        nc.vector.quantize_mx(out=qq_codes[:].bitcast(FP8X4), scales=qq_scales[:],
                              in_=qq[:].rearrange("p a w j -> p (a w j)"))

        lp = tile("lp", [P, T], F32, tag="dq_raw")
        lp_view = lp[:].rearrange("p (n c) -> p n c", n=P)
        for b in range(T // P // PACK):
            lp_ps = ps2.tile([P, PACK, P], F32, tag="bank_turn", name="lp_ps%d" % b)
            for c in range(PACK):
                col = PACK * b + c
                nc.tensor.transpose(lp_ps[:, c, :], lp_cols[:, col:col + 1].to_broadcast([P, P]), ident[:])
            nc.scalar.activation(out=lp_view[:, :, PACK * b:PACK * (b + 1)], in_=lp_ps[:].rearrange("p c n -> p n c"),
                                 func=ACT.Copy)

        a_ps = ps.tile([P, I], F32, tag="bank_a", name="a_ps")
        ta_ps = ps.tile([P, I], F32, tag="bank_ta", name="ta_ps")
        c_ps = ps.tile([P, I], F32, tag="bank_c", name="c_ps")
        for dst, half in ((a_ps, 0), (ta_ps, 1)):
            nc.tensor.matmul_mx(out=dst[:], lhsT=qq_codes[:, half * Q:(half + 1) * Q].bitcast(FP8X4),
                                lhsT_scale=qq_scales[:, half * Q:(half + 1) * Q],
                                rhs=kw_g[:].bitcast(FP4X4), rhs_scale=ks_g[:], start=True, stop=True)

        vs_g = tile("vs_g", [P, I], U8, tag="qq")
        nc.vector.tensor_copy(vs_g[:], vs[:].indirect(offsets[:]))
        nc.vector.tensor_copy(vw_g[:], vw[:].indirect(offsets[:]))

        go = tile("go", [P, Q, PACK], BF16)
        nc.scalar.copy(out=go[:], in_=go_raw[:].rearrange("p j w -> p w j"))
        neg_a = tile("neg_a", [P, I], F32)
        neg_max = tile("neg_max", [P, 1], F32)
        nc.vector.tensor_scalar(out=neg_a[:], in0=a_ps[:], scalar1=-1.0, scalar2=None, op0=ALU.mult, op1=ALU.min,
                                accum_out=neg_max[:])
        p_dealt = tile("p_dealt", [P, PACK, P], F32)
        p_sb = tile("p_sb", [P, I], F32)
        z = tile("z", [P, 1], F32)
        nc.scalar.activation(out=p_dealt[:], in_=a_ps[:].rearrange("p (s t) -> p t s", t=PACK), func=ACT.Exp,
                             bias=neg_max[:], scale=1.0, accum_out=z[:])
        nc.scalar.activation(out=p_sb[:], in_=a_ps[:], func=ACT.Exp, bias=neg_max[:], scale=1.0)

        go_codes = tile("go_codes", [P, Q], U32)
        go_scales = tile("go_scales", [P, Q], U8)
        nc.vector.quantize_mx(out=go_codes[:].bitcast(FP8X4), scales=go_scales[:],
                              in_=go[:].rearrange("p w j -> p (w j)"))
        nc.tensor.matmul_mx(out=c_ps[:], lhsT=go_codes[:].bitcast(FP8X4), lhsT_scale=go_scales[:],
                            rhs=vw_g[:].bitcast(FP4X4), rhs_scale=vs_g[:], start=True, stop=True)

        def slots_to_partitions(src_bf16, grouped, name):
            bank = ps2.tile([P, 2, P], F32, tag="bank_turn", name=name + "_ps")
            words = src_bf16[:].bitcast(F32)
            for u in range(2):
                nc.tensor.transpose(bank[:, u, :], words[:, u::2], ident[:])
            nc.scalar.copy(out=grouped.bitcast(F32), in_=bank[:].rearrange("p u r -> p r u"))

        def quantise(grouped, name, tag):
            width = grouped.shape[1] * P
            codes = tile(name + "_codes", [P, width], U32, tag=tag)
            scales = tile(name + "_scales", [P, width], U8)
            nc.vector.quantize_mx(out=codes[:].bitcast(FP8X4), scales=scales[:],
                                  in_=grouped[:].rearrange("p a r t -> p (a r t)"))
            return codes, scales

        def key_plane(j, grouped, tag=None):
            kt = tile("kt%d" % j, [P, I], BF16, tag=tag)
            nc.vector.tensor_copy(kt[:], kr[j][:].indirect(offsets[:]))
            slots_to_partitions(kt, grouped, "kt%d" % j)

        r = tile("r", [P, 1], F32)
        nc.vector.reciprocal(out=r[:], in_=z[:])
        nu = tile("nu", [P, I], F32)
        nc.vector.tensor_tensor(nu[:], lp[:].indirect(offsets[:]), neg_a[:], ALU.add)
        pi_ta = tile("pi_ta", [P, PACK, P], F32)
        m = tile("m", [P, 1], F32)
        nc.vector.scalar_tensor_tensor(out=pi_ta[:], in0=ta_ps[:].rearrange("p (s t) -> p t s", t=PACK), scalar=r[:],
                                       in1=p_dealt[:], op0=ALU.mult, op1=ALU.mult, accum_out=m[:])
        g = tile("g", [P, I], F32)
        nc.vector.scalar_tensor_tensor(out=g[:], in0=nu[:], scalar=s_col[:], in1=c_ps[:], op0=ALU.mult, op1=ALU.add)
        pi_g = tile("pi_g", [P, I], F32)
        g_bar = tile("g_bar", [P, 1], F32)
        nc.vector.scalar_tensor_tensor(out=pi_g[:], in0=g[:], scalar=r[:], in1=p_sb[:], op0=ALU.mult,
                                       op1=ALU.mult, accum_out=g_bar[:])
        last = tile("last", [P, 1, P, PACK], BF16)
        kr0_bf16 = tile("kr0_bf16", [P, T], BF16)
        nc.scalar.activation(out=kr0_bf16[:], in_=kr[0][:], func=ACT.Copy)
        kt0 = tile("kt0", [P, I], BF16)
        nc.scalar.activation(out=kt0[:], in_=kr0_bf16[:].indirect(offsets[:]), func=ACT.Copy)
        neg_r = tile("neg_r", [P, 1], F32)
        nc.gpsimd.tensor_scalar(out=neg_r[:], in0=r[:], scalar1=-1.0, scalar2=0.0, op0=ALU.mult, op1=ALU.add)
        mr = tile("mr", [P, 1], F32)
        nc.gpsimd.tensor_scalar(out=mr[:], in0=m[:], scalar1=r[:], scalar2=0.0, op0=ALU.mult, op1=ALU.add)
        neg_k = tile("neg_k", [P, 1], F32)
        nc.vector.tensor_scalar(out=neg_k[:], in0=g_bar[:], scalar1=s_col[:], scalar2=-1.0, op0=ALU.add, op1=ALU.mult)
        kmr = tile("kmr", [P, 1], F32)
        nc.vector.tensor_scalar(out=kmr[:], in0=g_bar[:], scalar1=s_col[:], scalar2=mr[:], op0=ALU.add, op1=ALU.mult)
        w = tile("w", [P, I], F32)
        cov = tile("cov", [P, 1], F32)
        nc.vector.scalar_tensor_tensor(out=w[:], in0=ta_ps[:], scalar=m[:], in1=pi_g[:], op0=ALU.subtract,
                                       op1=ALU.mult, accum_out=cov[:])
        term_ta = tile("term_ta", [P, PACK, P], F32)
        nc.scalar.activation(out=term_ta[:], in_=pi_ta[:], func=ACT.Copy, scale=neg_k[:])
        coef = tile("coef", [P, 1], F32)
        nc.scalar.activation(out=coef[:], in_=cov[:], func=ACT.Identity, bias=kmr[:], scale=neg_r[:])
        term_pi = tile("term_pi", [P, PACK, P], F32)
        nc.scalar.activation(out=term_pi[:], in_=p_dealt[:], func=ACT.Copy, scale=coef[:])

        first = tile("first", [P, 4, P, PACK], BF16, tag="p_dealt")
        slots_to_partitions(kt0, first[:, 1], "kt0")
        gt1 = tile("gt1", [P, PACK, Q], BF16)
        tdb_ps = [ps.tile([P, P], F32, tag=tag, name="tdb_ps%d" % t)
                  for t, tag in enumerate(("bank_a", "bank_c", "bank_x", "bank_ta"))]
        for t in range(PACK):
            nc.tensor.matmul(tdb_ps[t][:], w[:, t::PACK], ident[:], is_transpose=True, start=True, stop=False)
        for t in range(PACK):
            nc.tensor.matmul(tdb_ps[t][:], term_ta[:, t, :], ident[:], is_transpose=True, start=False, stop=False)
        for t in range(PACK):
            nc.tensor.matmul(tdb_ps[t][:], term_pi[:, t, :], ident[:], is_transpose=True, start=False, stop=True)
            nc.scalar.activation(out=gt1[:, t, :], in_=tdb_ps[t][:], func=ACT.Copy, scale=fs_col[:, t:t + 1])
        nc.scalar.copy(out=first[:, 0], in_=gt1[:].rearrange("p t q -> p q t"))
        key_plane(1, first[:, 2], "pi_g")
        key_plane(2, first[:, 3])
        key_plane(PLANES - 1, last[:, 0])
        first_codes, first_scales = quantise(first, "first", "kr3")
        last_codes, last_scales = quantise(last, "last", None)

        def product(acc, codes, scales):
            nc.tensor.matmul_mx(out=acc, lhsT=first_codes[:, 0:P].bitcast(FP8X4), lhsT_scale=first_scales[:, 0:P],
                                rhs=codes.bitcast(FP8X4), rhs_scale=scales, start=True, stop=True)

        def finish(acc, cols, name, tag=None):
            y = tile(name, [P, cols.stop - cols.start], F32, tag=tag)
            nc.vector.tensor_tensor(out=y[:], in0=acc[:], in1=res_sb[:, cols], op=ALU.add)
            nc.sync.dma_start(out=out[:, cols], in_=y[:])

        acc_head = ps.tile([P, 3 * P], F32, tag="bank_a", name="acc_head")
        product(acc_head[:, 0:P], first_codes[:, P:2 * P], first_scales[:, P:2 * P])
        product(acc_head[:, P:3 * P], first_codes[:, 2 * P:4 * P], first_scales[:, 2 * P:4 * P])
        finish(acc_head, slice(0, 3 * P), "y_head", "last")
        acc_tail = ps.tile([P, P], F32, tag="bank_c", name="acc_tail")
        product(acc_tail[:], last_codes[:], last_scales[:])
        finish(acc_tail, slice(3 * P, D), "y_tail")
